import numpy as np
import ml_dtypes


def mxq(x, axis, fmt="e4m3"):
    dtype, down = {"e4m3": (ml_dtypes.float8_e4m3fn, 7), "e5m2": (ml_dtypes.float8_e5m2, 14)}[fmt]
    v = np.moveaxis(np.asarray(x, np.float32).astype(ml_dtypes.bfloat16).astype(np.float64), axis, -1)
    blocks = v.reshape(v.shape[:-1] + (-1, 32))
    amax = np.abs(blocks).max(-1, keepdims=True)
    byte = np.maximum(np.where(amax > 0, np.frexp(amax)[1] - 1 + 127, 0) - down, 1)
    scale = np.exp2(byte - 127.0)
    codes = (blocks / scale).astype(np.float32).astype(dtype).astype(np.float64)
    return np.moveaxis((codes * scale).reshape(v.shape), -1, axis)


WIDE = False


def mx_kscale(k):
    if not WIDE:
        return np.ones(k)
    levels = np.array([10, -10, 5, -5, 0])
    if k % 512:
        return np.exp2(np.random.permutation(np.resize(levels, k // 32))).repeat(32)
    a = np.empty((k // 512, 16))
    for p in range(k // 512):
        a[p, :8] = np.random.permutation(np.resize(levels, 8))
        for g in range(8):
            far = levels[np.abs(levels - a[p, g]) >= 10]
            a[p, g + 8] = far[np.random.randint(len(far))]
    return np.exp2(a.ravel()).repeat(32)


def f64(x):
    return np.asarray(x).astype(np.float64)


def striped(idx):
    return np.tile(idx.reshape(-1, 16).T, (8, 1)).astype(np.uint16)


def unstriped(offs):
    return offs[:16].T.reshape(-1).astype(np.int64)


def relu(v):
    return np.maximum(v, 0.0)


K, T, E, C, N = 1024, 2048, 16, 256, 128


def by_expert(wq, xq):
    return np.concatenate([wq[e].T @ xq[:, e * C:(e + 1) * C] for e in range(E)], axis=1)


def setup_inputs():
    n = np.random.standard_normal
    s = mx_kscale(K)[:, None]
    first = np.random.permutation(np.repeat(np.arange(E), T // E))
    second = (first + 1 + np.random.permutation(np.repeat(np.arange(E - 1), -(-T // (E - 1)))[:T])) % E
    while np.bincount(second, minlength=E).max() != T // E:
        load = np.bincount(second, minlength=E); hi, lo = int(load.argmax()), int(load.argmin())
        t = np.flatnonzero((second == hi) & (first != lo))[0]; second[t] = lo
    slot_token = np.empty(E * C, np.int64); pos = np.empty((2, T), np.int64); fill = np.zeros(E, np.int64)
    place = np.stack([np.random.permutation(C) for _ in range(E)])
    for r, deal in enumerate((first, second)):
        for t in np.random.permutation(T):
            e = deal[t]; j = e * C + place[e, fill[e]]; fill[e] += 1; slot_token[j] = t; pos[r, t] = j
    g = np.random.uniform(0.2, 0.8, T)
    return {
        "xT": (n((K, T)) * s).astype(np.float32),
        "w": (n((E, K, N)) / np.sqrt(K) / s[None]).astype(np.float32),
        "b": (0.3 * n((N, E))).astype(np.float32),
        "gate": np.stack([np.tile(g, (N, 1)), np.tile(1.0 - g, (N, 1))]).astype(np.float32),
        "offs": striped(slot_token),
        "pos1": striped(pos[0]),
        "pos2": striped(pos[1]),
    }


def reference(xT, w, b, gate, offs, pos1, pos2):
    idx = unstriped(offs)
    xq = mxq(f64(xT)[:, idx], 0, "e4m3")
    y = by_expert(mxq(f64(w), 1, "e4m3"), xq)
    y = relu(y + np.repeat(f64(b), C, axis=1))
    return f64(gate[0]) * y[:, unstriped(pos1)] + f64(gate[1]) * y[:, unstriped(pos2)]

@@ -1,0 +1,163 @@
+from contextlib import ExitStack
+
+import concourse.mybir as mybir
+
+K, T, E, C, N = 1024, 2048, 16, 256, 128
+SLOTS = E * C
+FLOPS = 2 * K * N * SLOTS
+
+F32 = mybir.dt.float32
+BF16 = mybir.dt.bfloat16
+U32 = mybir.dt.uint32
+U16 = mybir.dt.uint16
+U8 = mybir.dt.uint8
+FP8X4 = mybir.dt.float8_e4m3fn_x4
+MULT, ADD = mybir.AluOpType.mult, mybir.AluOpType.add
+RELU = mybir.ActivationFunctionType.Relu
+
+P = 128
+PACK = 4
+K_PASS = P * PACK
+PASSES = K // K_PASS
+CHUNK = 512
+CHUNKS = T // CHUNK
+PAIR = 2
+W_TILES = E // PAIR
+GPSIMD_W = (2, 5)
+CUTS = ((0, 1024), (1024, 2048), (2048, 3072), (3072, 3584), (3584, 3840), (3840, 4096))
+
+
+def tile_routed_moe_kernel(tc, xT, w, b, gate, offs, pos1, pos2, out):
+    nc = tc.nc
+    with ExitStack() as ctx:
+        held = ctx.enter_context(tc.tile_pool(name="held", bufs=1))
+        rawp = ctx.enter_context(tc.tile_pool(name="rawp", bufs=12))
+        grpp = ctx.enter_context(tc.tile_pool(name="grpp", bufs=6))
+        gatp = ctx.enter_context(tc.tile_pool(name="gatp", bufs=3))
+        psum = ctx.enter_context(tc.psum_pool(name="psum", bufs=8))
+
+        offs_sb = held.tile([P, SLOTS // 16], U16, name="offs_sb")
+        pos1_sb = held.tile([P, T // 16], U16, name="pos1_sb")
+        pos2_sb = held.tile([P, T // 16], U16, name="pos2_sb")
+        bias = held.tile([P, E], F32, name="bias")
+        xw = [held.tile([P, T], U32, name=f"xw{a}", align_bytes=64) for a in range(PASSES)]
+        xs = held.tile([P, T], U8, name="xs", align_bytes=64)
+        gw0 = held.tile([P, SLOTS], U32, name="gw0", align_bytes=64)
+        wc = held.tile([P, E * PASSES * N], U32, name="wc", align_bytes=64)
+        ws = held.tile([P, E * PASSES * N], U8, name="ws", align_bytes=64)
+        y = held.tile([P, SLOTS], F32, name="y")
+        prod = [held.tile([P, T], F32, name=f"prod{r}") for r in range(2)]
+
+        nc.gpsimd.memset(xs[:], 0)
+
+        xv = xT.rearrange("(a p j) t -> a p j t", p=P, j=PACK)
+        wv = w.rearrange("e (a p j) n -> p e a (j n)", p=P, j=PACK)
+
+        raw = {}
+        for a in range(PASSES):
+            for c in range(CHUNKS):
+                t = rawp.tile([P, PACK, CHUNK], F32, name="raw", tag="raw")
+                nc.sync.dma_start(out=t[:], in_=xv[a, :, :, c * CHUNK : (c + 1) * CHUNK])
+                raw[a, c] = t
+                if a == 0 and c == 1:
+                    nc.sync.dma_start(out=offs_sb[:], in_=offs)
+        wraw = []
+        for i in range(W_TILES):
+            t = rawp.tile([P, PAIR, PASSES, PACK * N], F32, name="wraw", tag="raw")
+            nc.sync.dma_start(out=t[:], in_=wv[:, i * PAIR : (i + 1) * PAIR, :, :])
+            wraw.append(t)
+            if i == 3:
+                nc.sync.dma_start(out=bias[:], in_=b)
+        nc.sync.dma_start(out=pos1_sb[:], in_=pos1)
+        nc.sync.dma_start(out=pos2_sb[:], in_=pos2)
+        gates = []
+        for r in range(2):
+            t = rawp.tile([P, T], F32, name="gates", tag="raw")
+            nc.sync.dma_start(out=t[:], in_=gate[r, :, :])
+            gates.append(t)
+
+        split = {(0, 0): 0, (0, 1): 512, (0, 2): 512, (0, 3): 320,
+                 (1, 0): 0, (1, 1): 0, (1, 2): 0, (1, 3): 256}
+        def interleave_tokens(a, c):
+            g = grpp.tile([P, CHUNK, PACK], BF16, name="grp", tag="grp", align_bytes=64)
+            v = split[a, c]
+            src = raw[a, c][:].rearrange("p j t -> p t j")
+            if v > 0:
+                nc.vector.tensor_copy(out=g[:, :v, :], in_=src[:, :v, :])
+            if v < CHUNK:
+                nc.scalar.copy(out=g[:, v:, :], in_=src[:, v:, :])
+            return g
+
+        def quantise_tokens(a, c, g):
+            cols = slice(c * CHUNK, (c + 1) * CHUNK)
+            nc.vector.quantize_mx(
+                out=xw[a][:, cols].bitcast(FP8X4),
+                scales=xs[4 * a :, cols],
+                in_=g[:].rearrange("p t j -> p (t j)"),
+            )
+
+        wq = PAIR * PASSES * N
+
+        def interleave_weights(i):
+            g = grpp.tile([P, PAIR * PASSES, N, PACK], BF16, name="wgrp", tag="grp", align_bytes=64)
+            src = wraw[i][:].rearrange("p e a (j n) -> p (e a) n j", j=PACK)
+            if i in GPSIMD_W:
+                for q in range(PAIR * PASSES):
+                    nc.gpsimd.tensor_scalar(out=g[:, q, :, :], in0=src[:, q, :, :], scalar1=1.0, scalar2=0.0, op0=MULT, op1=ADD)
+            else:
+                nc.scalar.copy(out=g[:], in_=src)
+            return g
+
+        def quantise_weights(i, g):
+            nc.vector.quantize_mx(
+                out=wc[:, i * wq : (i + 1) * wq].bitcast(FP8X4),
+                scales=ws[:, i * wq : (i + 1) * wq],
+                in_=g[:].rearrange("p q n j -> p (q n j)"),
+            )
+
+        def gather(dst, window, s0, s1):
+            nc.vector.tensor_copy(dst, window[:].indirect(offs_sb[:, s0 // 16 : s1 // 16]))
+
+        for c in range(CHUNKS):
+            quantise_tokens(0, c, interleave_tokens(0, c))
+        for s0, s1 in ((0, 1536), (1536, 3072), (3072, 4096)):
+            gather(gw0[:, s0:s1], xw[0], s0, s1)
+        for c in range(CHUNKS):
+            quantise_tokens(1, c, interleave_tokens(1, c))
+
+        for s0, s1 in CUTS:
+            gs = gatp.tile([P, s1 - s0], U8, name="gs", tag="gs", align_bytes=64)
+            gw1 = gatp.tile([P, s1 - s0], U32, name="gw1", tag="gw1", align_bytes=64)
+            gather(gs[:], xs, s0, s1)
+            gather(gw1[:], xw[1], s0, s1)
+            for e in range(s0 // C, s1 // C):
+                if e % PAIR == 0:
+                    quantise_weights(e // PAIR, interleave_weights(e // PAIR))
+                    bank = psum.tile([P, PAIR * C], F32, name="bank", tag="bank")
+                sl = slice(e * C, (e + 1) * C)
+                cs = slice(e * C - s0, (e + 1) * C - s0)
+                hs = slice(e % PAIR * C, (e % PAIR + 1) * C)
+                for a in range(PASSES):
+                    wcols = slice((e * PASSES + a) * N, (e * PASSES + a + 1) * N)
+                    nc.tensor.matmul_mx(
+                        out=bank[:, hs],
+                        lhsT=wc[:, wcols].bitcast(FP8X4),
+                        lhsT_scale=ws[:, wcols],
+                        rhs=(gw0[:, sl] if a == 0 else gw1[:, cs]).bitcast(FP8X4),
+                        rhs_scale=gs[4 * a :, cs],
+                        start=(a == 0),
+                        stop=(a == PASSES - 1),
+                    )
+                nc.scalar.activation(out=y[:, sl], in_=bank[:, hs], func=RELU, bias=bias[:, e : e + 1], scale=1.0)
+
+        def combine(r, t0, t1):
+            pos = (pos1_sb, pos2_sb)[r]
+            nc.vector.tensor_tensor(prod[r][:, t0:t1], y[:].indirect(pos[:, t0 // 16 : t1 // 16]), gates[r][:, t0:t1], MULT)
+
+        for t0, t1 in ((0, 1024), (1024, 2048)):
+            combine(0, t0, t1)
+            for u0 in range(t0, t1, 512):
+                ts = slice(u0, u0 + 512)
+                combine(1, u0, u0 + 512)
+                nc.vector.tensor_tensor(prod[0][:, ts], prod[0][:, ts], prod[1][:, ts], ADD)
+                nc.sync.dma_start(out=out[:, ts], in_=prod[0][:, ts])

@@ -17,28 +17,32 @@ RELU = mybir.ActivationFunctionType.Relu
 
 P = 128
 PACK = 4
-K_PASS = P * PACK
-PASSES = K // K_PASS
-CHUNK = 512
-CHUNKS = T // CHUNK
+PASSES = 2
 PAIR = 2
 W_TILES = E // PAIR
-GPSIMD_W = (2, 5)
-CUTS = ((0, 1024), (1024, 2048), (2048, 3072), (3072, 3584), (3584, 3840), (3840, 4096))
+CUTS0 = ((0, 1536), (1536, 3072), (3072, 4096))
+CUTS1 = ((0, 1536), (1536, 3072), (3072, 4096))
+TCUTS = ((0, 512), (512, 1024), (1024, 1536), (1536, 1792), (1792, 2048))
+XQ = (
+    (0, 0, 512, 512), (0, 512, 1024, 160), (0, 1024, 1536, 336), (0, 1536, 2048, 336),
+    (1, 0, 512, 0), (1, 512, 1024, 0), (1, 1024, 1536, 0), (1, 1536, 2048, 0),
+)
+XTILES = ((0, 0, (1024,)), (0, 1024, (512, 512)), (1, 0, (512, 512)), (1, 1024, (512, 512)))
+WTILES = ((4,), (4,), (4,), (2, 2))
 
 
 def tile_routed_moe_kernel(tc, xT, w, b, gate, offs, pos1, pos2, out):
     nc = tc.nc
     with ExitStack() as ctx:
         held = ctx.enter_context(tc.tile_pool(name="held", bufs=1))
-        rawp = ctx.enter_context(tc.tile_pool(name="rawp", bufs=12))
+        rawp = ctx.enter_context(tc.tile_pool(name="rawp", bufs=5))
         grpp = ctx.enter_context(tc.tile_pool(name="grpp", bufs=6))
-        gatp = ctx.enter_context(tc.tile_pool(name="gatp", bufs=3))
+        gatp = ctx.enter_context(tc.tile_pool(name="gatp", bufs=2))
+        prodp = ctx.enter_context(tc.tile_pool(name="prodp", bufs=2))
         psum = ctx.enter_context(tc.psum_pool(name="psum", bufs=8))
 
         offs_sb = held.tile([P, SLOTS // 16], U16, name="offs_sb")
-        pos1_sb = held.tile([P, T // 16], U16, name="pos1_sb")
-        pos2_sb = held.tile([P, T // 16], U16, name="pos2_sb")
+        pos_sb = [held.tile([P, T // 16], U16, name=f"pos{r}_sb") for r in range(2)]
         bias = held.tile([P, E], F32, name="bias")
         xw = [held.tile([P, T], U32, name=f"xw{a}", align_bytes=64) for a in range(PASSES)]
         xs = held.tile([P, T], U8, name="xs", align_bytes=64)
@@ -46,93 +50,92 @@ def tile_routed_moe_kernel(tc, xT, w, b, gate, offs, pos1, pos2, out):
         wc = held.tile([P, E * PASSES * N], U32, name="wc", align_bytes=64)
         ws = held.tile([P, E * PASSES * N], U8, name="ws", align_bytes=64)
         y = held.tile([P, SLOTS], F32, name="y")
-        prod = [held.tile([P, T], F32, name=f"prod{r}") for r in range(2)]
 
         nc.gpsimd.memset(xs[:], 0)
 
         xv = xT.rearrange("(a p j) t -> a p j t", p=P, j=PACK)
         wv = w.rearrange("e (a p j) n -> p e a (j n)", p=P, j=PACK)
 
-        raw = {}
-        for a in range(PASSES):
-            for c in range(CHUNKS):
-                t = rawp.tile([P, PACK, CHUNK], F32, name="raw", tag="raw")
-                nc.sync.dma_start(out=t[:], in_=xv[a, :, :, c * CHUNK : (c + 1) * CHUNK])
-                raw[a, c] = t
-                if a == 0 and c == 1:
+        raw = []
+        for a, t0, loads in XTILES:
+            t = rawp.tile([P, PACK, 1024], F32, name="raw", tag="raw")
+            u0 = t0
+            for n in loads:
+                nc.sync.dma_start(out=t[:, :, u0 - t0 : u0 - t0 + n], in_=xv[a, :, :, u0 : u0 + n])
+                u0 += n
+                if (a, u0) == (0, 1536):
                     nc.sync.dma_start(out=offs_sb[:], in_=offs)
+            raw.append((a, t0, t0 + 1024, t))
         wraw = []
-        for i in range(W_TILES):
-            t = rawp.tile([P, PAIR, PASSES, PACK * N], F32, name="wraw", tag="raw")
-            nc.sync.dma_start(out=t[:], in_=wv[:, i * PAIR : (i + 1) * PAIR, :, :])
+        for i, loads in enumerate(WTILES):
+            t = rawp.tile([P, 4, PASSES, PACK * N], F32, name="wraw", tag="raw")
+            e = 0
+            for n in loads:
+                nc.sync.dma_start(out=t[:, e : e + n, :, :], in_=wv[:, i * 4 + e : i * 4 + e + n, :, :])
+                e += n
             wraw.append(t)
-            if i == 3:
-                nc.sync.dma_start(out=bias[:], in_=b)
-        nc.sync.dma_start(out=pos1_sb[:], in_=pos1)
-        nc.sync.dma_start(out=pos2_sb[:], in_=pos2)
-        gates = []
-        for r in range(2):
-            t = rawp.tile([P, T], F32, name="gates", tag="raw")
-            nc.sync.dma_start(out=t[:], in_=gate[r, :, :])
-            gates.append(t)
+        nc.sync.dma_start(out=bias[:], in_=b)
+        nc.sync.dma_start(out=pos_sb[0][:], in_=pos1)
+        nc.sync.dma_start(out=pos_sb[1][:], in_=pos2)
+        gates = rawp.tile([P, 2, T], F32, name="gates", tag="raw")
+        nc.sync.dma_start(out=gates[:], in_=gate.rearrange("r p t -> p r t"))
 
-        split = {(0, 0): 0, (0, 1): 512, (0, 2): 512, (0, 3): 320,
-                 (1, 0): 0, (1, 1): 0, (1, 2): 0, (1, 3): 256}
-        def interleave_tokens(a, c):
-            g = grpp.tile([P, CHUNK, PACK], BF16, name="grp", tag="grp", align_bytes=64)
-            v = split[a, c]
-            src = raw[a, c][:].rearrange("p j t -> p t j")
+        def tokens(a, t0, t1, v):
+            l0, src = [(u0, t) for b0, u0, u1, t in raw if b0 == a and u0 <= t0 and t1 <= u1][0]
+            g = grpp.tile([P, t1 - t0, PACK], BF16, name="grp", tag="grp", align_bytes=64)
+
+            def cut(c0, c1):
+                return (g[:, c0:c1, :].rearrange("p (c i) j -> p c j i", i=4),
+                        src[:, :, t0 - l0 + c0 : t0 - l0 + c1].rearrange("p j (c i) -> p c j i", i=4))
+
             if v > 0:
-                nc.vector.tensor_copy(out=g[:, :v, :], in_=src[:, :v, :])
-            if v < CHUNK:
-                nc.scalar.copy(out=g[:, v:, :], in_=src[:, v:, :])
-            return g
-
-        def quantise_tokens(a, c, g):
-            cols = slice(c * CHUNK, (c + 1) * CHUNK)
+                o, s = cut(0, v)
+                nc.vector.tensor_copy(out=o, in_=s)
+            if v < t1 - t0:
+                o, s = cut(v, t1 - t0)
+                nc.scalar.copy(out=o, in_=s)
             nc.vector.quantize_mx(
-                out=xw[a][:, cols].bitcast(FP8X4),
-                scales=xs[4 * a :, cols],
+                out=xw[a][:, t0:t1].bitcast(FP8X4),
+                scales=xs[4 * a :, t0:t1],
                 in_=g[:].rearrange("p t j -> p (t j)"),
             )
 
         wq = PAIR * PASSES * N
 
-        def interleave_weights(i):
+        def weights(i):
             g = grpp.tile([P, PAIR * PASSES, N, PACK], BF16, name="wgrp", tag="grp", align_bytes=64)
-            src = wraw[i][:].rearrange("p e a (j n) -> p (e a) n j", j=PACK)
-            if i in GPSIMD_W:
-                for q in range(PAIR * PASSES):
-                    nc.gpsimd.tensor_scalar(out=g[:, q, :, :], in0=src[:, q, :, :], scalar1=1.0, scalar2=0.0, op0=MULT, op1=ADD)
-            else:
-                nc.scalar.copy(out=g[:], in_=src)
-            return g
-
-        def quantise_weights(i, g):
-            nc.vector.quantize_mx(
-                out=wc[:, i * wq : (i + 1) * wq].bitcast(FP8X4),
-                scales=ws[:, i * wq : (i + 1) * wq],
-                in_=g[:].rearrange("p q n j -> p (q n j)"),
-            )
+            src = wraw[i // 2][:, i % 2 * 2 : i % 2 * 2 + 2, :, :].rearrange("p e a (j c i) -> p (e a) c j i", j=PACK, i=4)
+            nc.scalar.copy(out=g[:].rearrange("p q (c i) j -> p q c j i", i=4), in_=src)
+            parts = 2 if i == W_TILES - 1 else 1
+            for h in range(parts):
+                q = slice(i * wq + h * wq // parts, i * wq + (h + 1) * wq // parts)
+                m = PAIR * PASSES // parts
+                nc.vector.quantize_mx(
+                    out=wc[:, q].bitcast(FP8X4),
+                    scales=ws[:, q],
+                    in_=g[:, h * m : (h + 1) * m, :, :].rearrange("p q n j -> p (q n j)"),
+                )
 
         def gather(dst, window, s0, s1):
             nc.vector.tensor_copy(dst, window[:].indirect(offs_sb[:, s0 // 16 : s1 // 16]))
 
-        for c in range(CHUNKS):
-            quantise_tokens(0, c, interleave_tokens(0, c))
-        for s0, s1 in ((0, 1536), (1536, 3072), (3072, 4096)):
+        for a, t0, t1, v in XQ:
+            if a == 0:
+                tokens(a, t0, t1, v)
+        for s0, s1 in CUTS0:
             gather(gw0[:, s0:s1], xw[0], s0, s1)
-        for c in range(CHUNKS):
-            quantise_tokens(1, c, interleave_tokens(1, c))
+        for a, t0, t1, v in XQ:
+            if a == 1:
+                tokens(a, t0, t1, v)
 
-        for s0, s1 in CUTS:
+        for s0, s1 in CUTS1:
             gs = gatp.tile([P, s1 - s0], U8, name="gs", tag="gs", align_bytes=64)
             gw1 = gatp.tile([P, s1 - s0], U32, name="gw1", tag="gw1", align_bytes=64)
             gather(gs[:], xs, s0, s1)
             gather(gw1[:], xw[1], s0, s1)
             for e in range(s0 // C, s1 // C):
                 if e % PAIR == 0:
-                    quantise_weights(e // PAIR, interleave_weights(e // PAIR))
+                    weights(e // PAIR)
                     bank = psum.tile([P, PAIR * C], F32, name="bank", tag="bank")
                 sl = slice(e * C, (e + 1) * C)
                 cs = slice(e * C - s0, (e + 1) * C - s0)
@@ -150,14 +153,12 @@ def tile_routed_moe_kernel(tc, xT, w, b, gate, offs, pos1, pos2, out):
                     )
                 nc.scalar.activation(out=y[:, sl], in_=bank[:, hs], func=RELU, bias=bias[:, e : e + 1], scale=1.0)
 
-        def combine(r, t0, t1):
-            pos = (pos1_sb, pos2_sb)[r]
-            nc.vector.tensor_tensor(prod[r][:, t0:t1], y[:].indirect(pos[:, t0 // 16 : t1 // 16]), gates[r][:, t0:t1], MULT)
-
-        for t0, t1 in ((0, 1024), (1024, 2048)):
-            combine(0, t0, t1)
-            for u0 in range(t0, t1, 512):
-                ts = slice(u0, u0 + 512)
-                combine(1, u0, u0 + 512)
-                nc.vector.tensor_tensor(prod[0][:, ts], prod[0][:, ts], prod[1][:, ts], ADD)
-                nc.sync.dma_start(out=out[:, ts], in_=prod[0][:, ts])
+        for t0, t1 in TCUTS:
+            prod = []
+            for r in range(2):
+                p = prodp.tile([P, t1 - t0], F32, name=f"prod{r}", tag=f"prod{r}")
+                nc.vector.tensor_tensor(p[:], y[:].indirect(pos_sb[r][:, t0 // 16 : t1 // 16]), gates[:, r, t0:t1], MULT)
+                prod.append(p)
+            o = prodp.tile([P, t1 - t0], F32, name="o", tag="o")
+            nc.vector.tensor_tensor(o[:], prod[0][:], prod[1][:], ADD)
+            nc.sync.dma_start(out=out[:, t0:t1], in_=o[:])

@@ -1,6 +1,7 @@
 from contextlib import ExitStack
 
 import concourse.mybir as mybir
+from concourse.masks import make_identity
 
 K, T, E, C, N = 1024, 2048, 16, 256, 128
 SLOTS = E * C
@@ -22,12 +23,14 @@ PAIR = 2
 W_TILES = E // PAIR
 CUTS0 = ((0, 1536), (1536, 3072), (3072, 4096))
 CUTS1 = ((0, 1536), (1536, 3072), (3072, 4096))
-TCUTS = ((0, 512), (512, 1024), (1024, 1536), (1536, 1792), (1792, 2048))
+TCUTS_PE = ((0, 512), (512, 1024), (1024, 1536))
+TCUTS_V = ((1536, 1792), (1792, 2048))
+GPSIMD_W = ()
 XQ = (
-    (0, 0, 512, 512), (0, 512, 1024, 160), (0, 1024, 1536, 336), (0, 1536, 2048, 336),
+    (0, 0, 512, 512), (0, 512, 1024, 160), (0, 1024, 1536, 336), (0, 1536, 1792, 176), (0, 1792, 2048, 176),
     (1, 0, 512, 0), (1, 512, 1024, 0), (1, 1024, 1536, 0), (1, 1536, 2048, 0),
 )
-XTILES = ((0, 0, (1024,)), (0, 1024, (512, 512)), (1, 0, (512, 512)), (1, 1024, (512, 512)))
+XTILES = ((0, 0, (1024,)), (0, 1024, (512, 256, 256)), (1, 0, (512, 512)), (1, 1024, (512, 512)))
 WTILES = ((4,), (4,), (4,), (2, 2))
 
 
@@ -52,6 +55,8 @@ def tile_routed_moe_kernel(tc, xT, w, b, gate, offs, pos1, pos2, out):
         y = held.tile([P, SLOTS], F32, name="y")
 
         nc.gpsimd.memset(xs[:], 0)
+        ident = held.tile([P, P], F32, name="ident")
+        make_identity(nc, ident[:])
 
         xv = xT.rearrange("(a p j) t -> a p j t", p=P, j=PACK)
         wv = w.rearrange("e (a p j) n -> p e a (j n)", p=P, j=PACK)
@@ -105,7 +110,12 @@ def tile_routed_moe_kernel(tc, xT, w, b, gate, offs, pos1, pos2, out):
         def weights(i):
             g = grpp.tile([P, PAIR * PASSES, N, PACK], BF16, name="wgrp", tag="grp", align_bytes=64)
             src = wraw[i // 2][:, i % 2 * 2 : i % 2 * 2 + 2, :, :].rearrange("p e a (j c i) -> p (e a) c j i", j=PACK, i=4)
-            nc.scalar.copy(out=g[:].rearrange("p q (c i) j -> p q c j i", i=4), in_=src)
+            dst = g[:].rearrange("p q (c i) j -> p q c j i", i=4)
+            if i in GPSIMD_W:
+                for q in range(PAIR * PASSES):
+                    nc.gpsimd.tensor_scalar(out=dst[:, q], in0=src[:, q], scalar1=1.0, scalar2=0.0, op0=MULT, op1=ADD)
+            else:
+                nc.scalar.copy(out=dst, in_=src)
             parts = 2 if i == W_TILES - 1 else 1
             for h in range(parts):
                 q = slice(i * wq + h * wq // parts, i * wq + (h + 1) * wq // parts)
@@ -151,14 +161,29 @@ def tile_routed_moe_kernel(tc, xT, w, b, gate, offs, pos1, pos2, out):
                         start=(a == 0),
                         stop=(a == PASSES - 1),
                     )
-                nc.scalar.activation(out=y[:, sl], in_=bank[:, hs], func=RELU, bias=bias[:, e : e + 1], scale=1.0)
+                if e == E - 1:
+                    nc.vector.tensor_scalar(out=y[:, sl], in0=bank[:, hs], scalar1=bias[:, e : e + 1], scalar2=0.0, op0=ADD, op1=mybir.AluOpType.max)
+                else:
+                    nc.scalar.activation(out=y[:, sl], in_=bank[:, hs], func=RELU, bias=bias[:, e : e + 1], scale=1.0)
 
-        for t0, t1 in TCUTS:
+        def products(t0, t1, tag, bufs):
             prod = []
             for r in range(2):
-                p = prodp.tile([P, t1 - t0], F32, name=f"prod{r}", tag=f"prod{r}")
+                p = prodp.tile([P, t1 - t0], F32, name=f"prod{r}", tag=f"{tag}{r}", bufs=bufs)
                 nc.vector.tensor_tensor(p[:], y[:].indirect(pos_sb[r][:, t0 // 16 : t1 // 16]), gates[:, r, t0:t1], MULT)
                 prod.append(p)
-            o = prodp.tile([P, t1 - t0], F32, name="o", tag="o")
+            return prod
+
+        for t0, t1 in TCUTS_PE:
+            prod = products(t0, t1, "pe", 3)
+            total = psum.tile([P, PAIR * C], F32, name="total", tag="bank")
+            for r in range(2):
+                nc.tensor.matmul(total[:], ident[:], prod[r][:], start=(r == 0), stop=(r == 1))
+            o = prodp.tile([P, t1 - t0], F32, name="o", tag="o", bufs=3)
+            nc.scalar.copy(out=o[:], in_=total[:])
+            nc.sync.dma_start(out=out[:, t0:t1], in_=o[:])
+        for t0, t1 in TCUTS_V:
+            prod = products(t0, t1, "v", 2)
+            o = prodp.tile([P, t1 - t0], F32, name="ov", tag="ov", bufs=2)
             nc.vector.tensor_tensor(o[:], prod[0][:], prod[1][:], ADD)
             nc.sync.dma_start(out=out[:, t0:t1], in_=o[:])

from contextlib import ExitStack

import concourse.mybir as mybir
from concourse.masks import make_identity

K, T, E, C, N = 1024, 2048, 16, 256, 128
SLOTS = E * C
FLOPS = 2 * K * N * SLOTS

F32 = mybir.dt.float32
BF16 = mybir.dt.bfloat16
U32 = mybir.dt.uint32
U16 = mybir.dt.uint16
U8 = mybir.dt.uint8
FP8X4 = mybir.dt.float8_e4m3fn_x4
MULT, ADD = mybir.AluOpType.mult, mybir.AluOpType.add
RELU = mybir.ActivationFunctionType.Relu

P = 128
PACK = 4
PASSES = 2
PAIR = 2
W_TILES = E // PAIR
CUTS0 = ((0, 1536), (1536, 3072), (3072, 4096))
CUTS1 = ((0, 1536), (1536, 3072), (3072, 4096))
TCUTS_PE = ((0, 512), (512, 1024), (1024, 1536))
TCUTS_V = ((1536, 1792), (1792, 2048))
GPSIMD_W = ()
XQ = (
    (0, 0, 512, 512), (0, 512, 1024, 160), (0, 1024, 1536, 336), (0, 1536, 1792, 176), (0, 1792, 2048, 176),
    (1, 0, 512, 0), (1, 512, 1024, 0), (1, 1024, 1536, 0), (1, 1536, 2048, 0),
)
XTILES = ((0, 0, (1024,)), (0, 1024, (512, 256, 256)), (1, 0, (512, 512)), (1, 1024, (512, 512)))
WTILES = ((4,), (4,), (4,), (2, 2))


def tile_routed_moe_kernel(tc, xT, w, b, gate, offs, pos1, pos2, out):
    nc = tc.nc
    with ExitStack() as ctx:
        held = ctx.enter_context(tc.tile_pool(name="held", bufs=1))
        rawp = ctx.enter_context(tc.tile_pool(name="rawp", bufs=5))
        grpp = ctx.enter_context(tc.tile_pool(name="grpp", bufs=6))
        gatp = ctx.enter_context(tc.tile_pool(name="gatp", bufs=2))
        prodp = ctx.enter_context(tc.tile_pool(name="prodp", bufs=2))
        psum = ctx.enter_context(tc.psum_pool(name="psum", bufs=8))

        offs_sb = held.tile([P, SLOTS // 16], U16, name="offs_sb")
        pos_sb = [held.tile([P, T // 16], U16, name=f"pos{r}_sb") for r in range(2)]
        bias = held.tile([P, E], F32, name="bias")
        xw = [held.tile([P, T], U32, name=f"xw{a}", align_bytes=64) for a in range(PASSES)]
        xs = held.tile([P, T], U8, name="xs", align_bytes=64)
        gw0 = held.tile([P, SLOTS], U32, name="gw0", align_bytes=64)
        wc = held.tile([P, E * PASSES * N], U32, name="wc", align_bytes=64)
        ws = held.tile([P, E * PASSES * N], U8, name="ws", align_bytes=64)
        y = held.tile([P, SLOTS], F32, name="y")

        nc.gpsimd.memset(xs[:], 0)
        ident = held.tile([P, P], F32, name="ident")
        make_identity(nc, ident[:])

        xv = xT.rearrange("(a p j) t -> a p j t", p=P, j=PACK)
        wv = w.rearrange("e (a p j) n -> p e a (j n)", p=P, j=PACK)

        raw = []
        for a, t0, loads in XTILES:
            t = rawp.tile([P, PACK, 1024], F32, name="raw", tag="raw")
            u0 = t0
            for n in loads:
                nc.sync.dma_start(out=t[:, :, u0 - t0 : u0 - t0 + n], in_=xv[a, :, :, u0 : u0 + n])
                u0 += n
                if (a, u0) == (0, 1536):
                    nc.sync.dma_start(out=offs_sb[:], in_=offs)
            raw.append((a, t0, t0 + 1024, t))
        wraw = []
        for i, loads in enumerate(WTILES):
            t = rawp.tile([P, 4, PASSES, PACK * N], F32, name="wraw", tag="raw")
            e = 0
            for n in loads:
                nc.sync.dma_start(out=t[:, e : e + n, :, :], in_=wv[:, i * 4 + e : i * 4 + e + n, :, :])
                e += n
            wraw.append(t)
        nc.sync.dma_start(out=bias[:], in_=b)
        nc.sync.dma_start(out=pos_sb[0][:], in_=pos1)
        nc.sync.dma_start(out=pos_sb[1][:], in_=pos2)
        gates = rawp.tile([P, 2, T], F32, name="gates", tag="raw")
        nc.sync.dma_start(out=gates[:], in_=gate.rearrange("r p t -> p r t"))

        def tokens(a, t0, t1, v):
            l0, src = [(u0, t) for b0, u0, u1, t in raw if b0 == a and u0 <= t0 and t1 <= u1][0]
            g = grpp.tile([P, t1 - t0, PACK], BF16, name="grp", tag="grp", align_bytes=64)

            def cut(c0, c1):
                return (g[:, c0:c1, :].rearrange("p (c i) j -> p c j i", i=4),
                        src[:, :, t0 - l0 + c0 : t0 - l0 + c1].rearrange("p j (c i) -> p c j i", i=4))

            if v > 0:
                o, s = cut(0, v)
                nc.vector.tensor_copy(out=o, in_=s)
            if v < t1 - t0:
                o, s = cut(v, t1 - t0)
                nc.scalar.copy(out=o, in_=s)
            nc.vector.quantize_mx(
                out=xw[a][:, t0:t1].bitcast(FP8X4),
                scales=xs[4 * a :, t0:t1],
                in_=g[:].rearrange("p t j -> p (t j)"),
            )

        wq = PAIR * PASSES * N

        def weights(i):
            g = grpp.tile([P, PAIR * PASSES, N, PACK], BF16, name="wgrp", tag="grp", align_bytes=64)
            src = wraw[i // 2][:, i % 2 * 2 : i % 2 * 2 + 2, :, :].rearrange("p e a (j c i) -> p (e a) c j i", j=PACK, i=4)
            dst = g[:].rearrange("p q (c i) j -> p q c j i", i=4)
            if i in GPSIMD_W:
                for q in range(PAIR * PASSES):
                    nc.gpsimd.tensor_scalar(out=dst[:, q], in0=src[:, q], scalar1=1.0, scalar2=0.0, op0=MULT, op1=ADD)
            else:
                nc.scalar.copy(out=dst, in_=src)
            parts = 2 if i == W_TILES - 1 else 1
            for h in range(parts):
                q = slice(i * wq + h * wq // parts, i * wq + (h + 1) * wq // parts)
                m = PAIR * PASSES // parts
                nc.vector.quantize_mx(
                    out=wc[:, q].bitcast(FP8X4),
                    scales=ws[:, q],
                    in_=g[:, h * m : (h + 1) * m, :, :].rearrange("p q n j -> p (q n j)"),
                )

        def gather(dst, window, s0, s1):
            nc.vector.tensor_copy(dst, window[:].indirect(offs_sb[:, s0 // 16 : s1 // 16]))

        for a, t0, t1, v in XQ:
            if a == 0:
                tokens(a, t0, t1, v)
        for s0, s1 in CUTS0:
            gather(gw0[:, s0:s1], xw[0], s0, s1)
        for a, t0, t1, v in XQ:
            if a == 1:
                tokens(a, t0, t1, v)

        for s0, s1 in CUTS1:
            gs = gatp.tile([P, s1 - s0], U8, name="gs", tag="gs", align_bytes=64)
            gw1 = gatp.tile([P, s1 - s0], U32, name="gw1", tag="gw1", align_bytes=64)
            gather(gs[:], xs, s0, s1)
            gather(gw1[:], xw[1], s0, s1)
            for e in range(s0 // C, s1 // C):
                if e % PAIR == 0:
                    weights(e // PAIR)
                    bank = psum.tile([P, PAIR * C], F32, name="bank", tag="bank")
                sl = slice(e * C, (e + 1) * C)
                cs = slice(e * C - s0, (e + 1) * C - s0)
                hs = slice(e % PAIR * C, (e % PAIR + 1) * C)
                for a in range(PASSES):
                    wcols = slice((e * PASSES + a) * N, (e * PASSES + a + 1) * N)
                    nc.tensor.matmul_mx(
                        out=bank[:, hs],
                        lhsT=wc[:, wcols].bitcast(FP8X4),
                        lhsT_scale=ws[:, wcols],
                        rhs=(gw0[:, sl] if a == 0 else gw1[:, cs]).bitcast(FP8X4),
                        rhs_scale=gs[4 * a :, cs],
                        start=(a == 0),
                        stop=(a == PASSES - 1),
                    )
                if e == E - 1:
                    nc.vector.tensor_scalar(out=y[:, sl], in0=bank[:, hs], scalar1=bias[:, e : e + 1], scalar2=0.0, op0=ADD, op1=mybir.AluOpType.max)
                else:
                    nc.scalar.activation(out=y[:, sl], in_=bank[:, hs], func=RELU, bias=bias[:, e : e + 1], scale=1.0)

        def products(t0, t1, tag, bufs):
            prod = []
            for r in range(2):
                p = prodp.tile([P, t1 - t0], F32, name=f"prod{r}", tag=f"{tag}{r}", bufs=bufs)
                nc.vector.tensor_tensor(p[:], y[:].indirect(pos_sb[r][:, t0 // 16 : t1 // 16]), gates[:, r, t0:t1], MULT)
                prod.append(p)
            return prod

        for t0, t1 in TCUTS_PE:
            prod = products(t0, t1, "pe", 3)
            total = psum.tile([P, PAIR * C], F32, name="total", tag="bank")
            for r in range(2):
                nc.tensor.matmul(total[:], ident[:], prod[r][:], start=(r == 0), stop=(r == 1))
            o = prodp.tile([P, t1 - t0], F32, name="o", tag="o", bufs=3)
            nc.scalar.copy(out=o[:], in_=total[:])
            nc.sync.dma_start(out=out[:, t0:t1], in_=o[:])
        for t0, t1 in TCUTS_V:
            prod = products(t0, t1, "v", 2)
            o = prodp.tile([P, t1 - t0], F32, name="ov", tag="ov", bufs=2)
            nc.vector.tensor_tensor(o[:], prod[0][:], prod[1][:], ADD)
            nc.sync.dma_start(out=out[:, t0:t1], in_=o[:])
